import numpy as np
import ml_dtypes


def mxq(x, axis, fmt="e4m3"):
    dtype, down = {"e4m3": (ml_dtypes.float8_e4m3fn, 7), "e5m2": (ml_dtypes.float8_e5m2, 14)}[fmt]
    v = np.moveaxis(np.asarray(x, np.float32).astype(ml_dtypes.bfloat16).astype(np.float64), axis, -1)
    blocks = v.reshape(v.shape[:-1] + (-1, 32))
    amax = np.abs(blocks).max(-1, keepdims=True)
    byte = np.maximum(np.where(amax > 0, np.frexp(amax)[1] - 1 + 127, 0) - down, 1)
    scale = np.exp2(byte - 127.0)
    codes = (blocks / scale).astype(np.float32).astype(dtype).astype(np.float64)
    return np.moveaxis((codes * scale).reshape(v.shape), -1, axis)


WIDE = False


def mx_kscale(k):
    if not WIDE:
        return np.ones(k)
    levels = np.array([10, -10, 5, -5, 0])
    if k % 512:
        return np.exp2(np.random.permutation(np.resize(levels, k // 32))).repeat(32)
    a = np.empty((k // 512, 16))
    for p in range(k // 512):
        a[p, :8] = np.random.permutation(np.resize(levels, 8))
        for g in range(8):
            far = levels[np.abs(levels - a[p, g]) >= 10]
            a[p, g + 8] = far[np.random.randint(len(far))]
    return np.exp2(a.ravel()).repeat(32)


def f64(x):
    return np.asarray(x).astype(np.float64)


def striped(idx):
    return np.tile(idx.reshape(-1, 16).T, (8, 1)).astype(np.uint16)


def unstriped(offs):
    return offs[:16].T.reshape(-1).astype(np.int64)


def gelu(v):
    return 0.5 * v * (1.0 + np.tanh(np.sqrt(2.0 / np.pi) * (v + 0.044715 * v**3)))


K, T, E, C, H, N = 1024, 512, 4, 256, 512, 128


def by_expert(wq, xq):
    return np.concatenate([wq[e].T @ xq[:, e * C:(e + 1) * C] for e in range(E)], axis=1)


def setup_inputs():
    n = np.random.standard_normal
    s = mx_kscale(K)[:, None]
    u = mx_kscale(H)
    first = np.random.permutation(np.repeat(np.arange(E), T // E))
    second = (first + 1 + np.random.permutation(np.repeat(np.arange(E - 1), -(-T // (E - 1)))[:T])) % E
    while np.bincount(second, minlength=E).max() != T // E:
        load = np.bincount(second, minlength=E); hi, lo = int(load.argmax()), int(load.argmin())
        t = np.flatnonzero((second == hi) & (first != lo))[0]; second[t] = lo
    slot_token = np.empty(E * C, np.int64); pos = np.empty((2, T), np.int64); fill = np.zeros(E, np.int64)
    place = np.stack([np.random.permutation(C) for _ in range(E)])
    for r, deal in enumerate((first, second)):
        for t in np.random.permutation(T):
            e = deal[t]; j = e * C + place[e, fill[e]]; fill[e] += 1; slot_token[j] = t; pos[r, t] = j
    g = np.random.uniform(0.2, 0.8, T)
    return {
        "xT": (n((K, T)) * s).astype(np.float32),
        "w1": (n((E, K, H)) / np.sqrt(K) / s[None]).astype(np.float32),
        "w3": (n((E, K, H)) / np.sqrt(K) / s[None] * u[None, None, :]).astype(np.float32),
        "w2": (n((E, H, N)) / np.sqrt(H) / u[None, :, None]).astype(np.float32),
        "gate": np.stack([np.tile(g, (N, 1)), np.tile(1.0 - g, (N, 1))]).astype(np.float32),
        "offs": striped(slot_token),
        "pos1": striped(pos[0]),
        "pos2": striped(pos[1]),
    }


def reference(xT, w1, w3, w2, gate, offs, pos1, pos2):
    idx = unstriped(offs)
    xq = mxq(f64(xT)[:, idx], 0, "e4m3")
    h = gelu(by_expert(mxq(f64(w1), 1, "e4m3"), xq))
    h = h * by_expert(mxq(f64(w3), 1, "e4m3"), xq)
    y = by_expert(mxq(f64(w2), 1, "e4m3"), mxq(h, 0, "e4m3"))
    return f64(gate[0]) * y[:, unstriped(pos1)] + f64(gate[1]) * y[:, unstriped(pos2)]

@@ -1,0 +1,235 @@
+from contextlib import ExitStack
+
+import concourse.mybir as mybir
+
+K, T, E, C, H, N = 1024, 512, 4, 256, 512, 128
+FLOPS = 2 * E * C * (2 * K * H + H * N)
+
+F32 = mybir.dt.float32
+BF16 = mybir.dt.bfloat16
+U32 = mybir.dt.uint32
+U16 = mybir.dt.uint16
+U8 = mybir.dt.uint8
+FP8X4 = mybir.dt.float8_e4m3fn_x4
+GELU = mybir.ActivationFunctionType.Gelu_apprx_tanh
+MULT = mybir.AluOpType.mult
+ADD = mybir.AluOpType.add
+
+P = 128
+PACK = 4
+K_PASS = P * PACK
+PASSES = K // K_PASS
+HALF = 128
+UNITS = 4 * E
+RAW_BUFS = 12
+STAGE_BUFS = 8
+XS = 44
+GELU_LAG = 3
+MULT_LAG = 5
+
+
+def tile_routed_moe_kernel(tc, xT, w1, w3, w2, gate, offs, pos1, pos2, out):
+    nc = tc.nc
+    with ExitStack() as ctx:
+        lists = ctx.enter_context(tc.tile_pool(name="lists", bufs=1))
+        keep = ctx.enter_context(tc.tile_pool(name="keep", bufs=1))
+        ring = ctx.enter_context(tc.tile_pool(name="ring", bufs=RAW_BUFS))
+        stage = ctx.enter_context(tc.tile_pool(name="stage", bufs=STAGE_BUFS))
+        hidden = ctx.enter_context(tc.tile_pool(name="hidden", bufs=2))
+        psum = ctx.enter_context(tc.psum_pool(name="psum", bufs=2))
+
+        offs_t = lists.tile([P, E * C // 16], U16, name="offs_t")
+        nc.sync.dma_start(offs_t[:], offs)
+        pos1_t = lists.tile([P, T // 16], U16, name="pos1_t")
+        pos2_t = lists.tile([P, T // 16], U16, name="pos2_t")
+
+        x_view = xT.rearrange("(g p j) n -> g p j n", p=P, j=PACK)
+        w_views = (
+            w1.rearrange("e (g p j) c -> e g p j c", p=P, j=PACK),
+            w3.rearrange("e (g p j) c -> e g p j c", p=P, j=PACK),
+        )
+        sources = [x_view[g] for g in range(PASSES)]
+        for e in range(E):
+            for kind in range(2):
+                for g in range(PASSES):
+                    sources.append(w_views[kind][e, g])
+        sources.append(w2.rearrange("e (p j) n -> p e (j n)", j=PACK))
+        raws = []
+        gates = []
+
+        def issue():
+            if len(raws) < len(sources):
+                raw = ring.tile([P, PACK, 512], F32, name="raw", tag="raw")
+                nc.sync.dma_start(out=raw[:], in_=sources[len(raws)])
+                raws.append(raw)
+                if len(raws) == len(sources):
+                    nc.sync.dma_start(pos1_t[:], pos1)
+                    nc.sync.dma_start(pos2_t[:], pos2)
+                    gate_t = ring.tile([P, 2, T], F32, name="raw", tag="raw")
+                    nc.sync.dma_start(out=gate_t[:], in_=gate.rearrange("r n t -> n r t"))
+                    gates.append(gate_t)
+
+        for i in range(RAW_BUFS):
+            issue()
+
+        warm_in = keep.tile([P, 1], F32, name="warm_in")
+        warm_out = keep.tile([P, 1], F32, name="warm_out")
+        nc.vector.memset(warm_in[:], 0.0)
+        nc.scalar.activation(out=warm_out[:], in_=warm_in[:], func=GELU)
+
+        xw = [keep.tile([P, T], U32, name="xw%d" % g, align_bytes=64) for g in range(PASSES)]
+        xs = [keep.tile([P, T], U8, name="xs%d" % g, align_bytes=64) for g in range(PASSES)]
+        chain = ctx.enter_context(tc.tile_pool(name="chain", bufs=1))
+        gw = {}
+        gs = {}
+        for g in range(PASSES):
+            nc.gpsimd.memset(xs[g][:], 0)
+
+        for g in range(PASSES):
+            grouped = stage.tile([P, PACK * T], BF16, name="grouped", tag="grouped", align_bytes=64)
+            src = raws[g][:].rearrange("p j (c i) -> p c j i", i=4)
+            dst = grouped[:].rearrange("p (c i j) -> p c j i", i=4, j=PACK)
+            nc.scalar.copy(out=dst[:, :XS], in_=src[:, :XS])
+            nc.vector.tensor_copy(out=dst[:, XS:], in_=src[:, XS:])
+            nc.vector.quantize_mx(out=xw[g][:].bitcast(FP8X4), scales=xs[g][:], in_=grouped[:])
+            issue()
+
+        def gather_expert(e):
+            entries = offs_t[:, e * C // 16 : (e + 1) * C // 16]
+            gw[e] = chain.tile([P, PASSES, C], U32, name="gw", tag="lo%d" % ((e + 1) % 2), align_bytes=64)
+            gs[e] = chain.tile([P, PASSES, C], U8, name="gs", tag="hi%d" % ((e + 1) % 2), align_bytes=64)
+            for g in range(PASSES):
+                nc.vector.tensor_copy(out=gw[e][:, g, :], in_=xw[g][:].indirect(entries))
+            for g in range(PASSES):
+                nc.vector.tensor_copy(out=gs[e][:, g, :], in_=xs[g][:].indirect(entries))
+
+        wc = [keep.tile([P, H], U32, name="wc%d" % u, align_bytes=64) for u in range(UNITS)]
+        ws = [keep.tile([P, H], U8, name="ws%d" % u, align_bytes=64) for u in range(UNITS)]
+        hc = [keep.tile([P, C], U32, name="hc%d" % e, align_bytes=64) for e in range(E)]
+        hs = [keep.tile([P, C], U8, name="hs%d" % e, align_bytes=64) for e in range(E)]
+        groupeds = {}
+        banks = {}
+        gelus = {}
+        hbs = {}
+
+        def copy_unit(u):
+            src = raws[PASSES + u][:].rearrange("p j (m t) -> p m j t", t=4)
+            if u % 4 < 3:
+                grouped = stage.tile([P, PACK * H], BF16, name="grouped", tag="grouped", align_bytes=64)
+                nc.scalar.copy(out=grouped[:].rearrange("p (t m j) -> p m j t", t=4, j=PACK), in_=src)
+                groupeds[u] = [grouped]
+            else:
+                parity = (u // 4) % 2
+                groupeds[u] = []
+                for half in range(2):
+                    part = chain.tile(
+                        [P, PACK * H // 2], BF16, name="part", tag=("lo%d", "hi%d")[half] % parity, align_bytes=64
+                    )
+                    nc.vector.tensor_copy(
+                        out=part[:].rearrange("p (t m j) -> p m j t", t=2, j=PACK), in_=src[:, :, :, 2 * half : 2 * half + 2]
+                    )
+                    groupeds[u].append(part)
+            issue()
+
+        def quantize_unit(u):
+            width = H // len(groupeds[u])
+            for i, part in enumerate(groupeds[u]):
+                cols = slice(i * width, (i + 1) * width)
+                nc.vector.quantize_mx(out=wc[u][:, cols].bitcast(FP8X4), scales=ws[u][:, cols], in_=part[:])
+
+        def first_layer(e, kind):
+            for s in range(2):
+                acc = psum.tile([P, 4, HALF], F32, name="acc%d" % kind, tag="acc%d" % kind)
+                banks[(e, kind, s)] = acc
+                cols = slice(s * HALF, (s + 1) * HALF)
+                for t in range(4):
+                    chans = slice(t * P, (t + 1) * P)
+                    for g in range(PASSES):
+                        u = 4 * e + 2 * kind + g
+                        nc.tensor.matmul_mx(
+                            out=acc[:, t, :],
+                            lhsT=wc[u][:, chans].bitcast(FP8X4),
+                            lhsT_scale=ws[u][:, chans],
+                            rhs=gw[e][:, g, cols].bitcast(FP8X4),
+                            rhs_scale=gs[e][:, g, cols],
+                            start=(g == 0),
+                            stop=(g == PASSES - 1),
+                        )
+
+        def gelu(e, s):
+            ga = hidden.tile([P, HALF, 4], F32, name="ga", tag="ga", bufs=4)
+            nc.scalar.activation(out=ga[:], in_=banks[(e, 0, s)][:].rearrange("p t n -> p n t"), func=GELU)
+            gelus[(e, s)] = ga
+
+        def product(e, s):
+            if s == 0:
+                hbs[e] = hidden.tile([P, C, 4], BF16, name="hb", tag="hb", align_bytes=64)
+            nc.vector.tensor_tensor(
+                out=hbs[e][:, s * HALF : (s + 1) * HALF, :],
+                in0=banks[(e, 1, s)][:].rearrange("p t n -> p n t"),
+                in1=gelus[(e, s)][:],
+                op=MULT,
+            )
+
+        def quantize_hidden(e):
+            nc.vector.quantize_mx(
+                out=hc[e][:].bitcast(FP8X4), scales=hs[e][:], in_=hbs[e][:].rearrange("p n t -> p (n t)")
+            )
+
+        w2c = keep.tile([P, E * N], U32, name="w2c", align_bytes=64)
+        w2s = keep.tile([P, E * N], U8, name="w2s", align_bytes=64)
+
+        def second_weights():
+            grouped2 = stage.tile([P, PACK * E * N], BF16, name="grouped", tag="grouped", align_bytes=64)
+            src2 = raws[PASSES + UNITS][:].rearrange("p e (j c i) -> p e c j i", j=PACK, i=4)
+            dst2 = grouped2[:].rearrange("p (e c i j) -> p e c j i", e=E, i=4, j=PACK)
+            nc.scalar.copy(out=dst2[:, :2], in_=src2[:, :2])
+            nc.vector.tensor_copy(out=dst2[:, 2:], in_=src2[:, 2:])
+            nc.vector.quantize_mx(out=w2c[:].bitcast(FP8X4), scales=w2s[:], in_=grouped2[:])
+
+        gather_expert(0)
+
+        for u in range(UNITS + MULT_LAG):
+            if u < UNITS:
+                copy_unit(u)
+            if 1 <= u <= UNITS:
+                quantize_unit(u - 1)
+                if (u - 1) % 4 == 1:
+                    first_layer((u - 1) // 4, 0)
+                if (u - 1) % 4 == 3:
+                    first_layer((u - 1) // 4, 1)
+                    if (u - 1) // 4 + 1 < E:
+                        gather_expert((u - 1) // 4 + 1)
+            if u == UNITS:
+                second_weights()
+            if u >= GELU_LAG and (u - GELU_LAG) % 4 == 0 and (u - GELU_LAG) // 4 < E:
+                gelu((u - GELU_LAG) // 4, 0)
+                gelu((u - GELU_LAG) // 4, 1)
+            if u >= MULT_LAG and (u - MULT_LAG) % 4 == 0:
+                product((u - MULT_LAG) // 4, 0)
+            if u >= MULT_LAG + 1 and (u - MULT_LAG - 1) % 4 == 0:
+                product((u - MULT_LAG - 1) // 4, 1)
+            if u >= MULT_LAG + 2 and (u - MULT_LAG - 2) % 4 == 0:
+                quantize_hidden((u - MULT_LAG - 2) // 4)
+
+        y_sb = keep.tile([P, E * C], F32, name="y_sb")
+        for e in range(E):
+            y_ps = psum.tile([P, C], F32, name="y_ps", tag="y_ps")
+            nc.tensor.matmul_mx(
+                out=y_ps[:],
+                lhsT=w2c[:, e * N : (e + 1) * N].bitcast(FP8X4),
+                lhsT_scale=w2s[:, e * N : (e + 1) * N],
+                rhs=hc[e][:].bitcast(FP8X4),
+                rhs_scale=hs[e][:],
+                start=True,
+                stop=True,
+            )
+            nc.scalar.copy(out=y_sb[:, e * C : (e + 1) * C], in_=y_ps[:])
+
+        first = keep.tile([P, T], F32, name="first")
+        second = keep.tile([P, T], F32, name="second")
+        total = keep.tile([P, T], F32, name="total")
+        nc.vector.tensor_tensor(out=first[:], in0=y_sb[:].indirect(pos1_t[:]), in1=gates[0][:, 0, :], op=MULT)
+        nc.vector.tensor_tensor(out=second[:], in0=y_sb[:].indirect(pos2_t[:]), in1=gates[0][:, 1, :], op=MULT)
+        nc.vector.tensor_tensor(out=total[:], in0=first[:], in1=second[:], op=ADD)
+        nc.sync.dma_start(out=out, in_=total[:])

@@ -26,6 +26,7 @@ STAGE_BUFS = 8
 XS = 44
 GELU_LAG = 3
 MULT_LAG = 5
+V_THIRD = True
 
 
 def tile_routed_moe_kernel(tc, xT, w1, w3, w2, gate, offs, pos1, pos2, out):
@@ -108,34 +109,43 @@ def tile_routed_moe_kernel(tc, xT, w1, w3, w2, gate, offs, pos1, pos2, out):
         hc = [keep.tile([P, C], U32, name="hc%d" % e, align_bytes=64) for e in range(E)]
         hs = [keep.tile([P, C], U8, name="hs%d" % e, align_bytes=64) for e in range(E)]
         groupeds = {}
+        pairs = {}
         banks = {}
         gelus = {}
         hbs = {}
 
         def copy_unit(u):
             src = raws[PASSES + u][:].rearrange("p j (m t) -> p m j t", t=4)
-            if u % 4 < 3:
+            e, r = divmod(u, 4)
+            if r < 2:
                 grouped = stage.tile([P, PACK * H], BF16, name="grouped", tag="grouped", align_bytes=64)
                 nc.scalar.copy(out=grouped[:].rearrange("p (t m j) -> p m j t", t=4, j=PACK), in_=src)
-                groupeds[u] = [grouped]
+                groupeds[u] = grouped
             else:
-                parity = (u // 4) % 2
-                groupeds[u] = []
+                g = r - 2
+                if g == 0:
+                    pairs[e] = [
+                        chain.tile([P, PACK * H], BF16, name="pair", tag=("lo%d", "hi%d")[half] % (e % 2), align_bytes=64)
+                        for half in range(2)
+                    ]
                 for half in range(2):
-                    part = chain.tile(
-                        [P, PACK * H // 2], BF16, name="part", tag=("lo%d", "hi%d")[half] % parity, align_bytes=64
+                    engine_copy = nc.vector.tensor_copy if (g == 1 or (half == 0 and V_THIRD)) else nc.scalar.copy
+                    engine_copy(
+                        out=pairs[e][half][:, g * PACK * H // 2 : (g + 1) * PACK * H // 2].rearrange(
+                            "p (t m j) -> p m j t", t=2, j=PACK
+                        ),
+                        in_=src[:, :, :, 2 * half : 2 * half + 2],
                     )
-                    nc.vector.tensor_copy(
-                        out=part[:].rearrange("p (t m j) -> p m j t", t=2, j=PACK), in_=src[:, :, :, 2 * half : 2 * half + 2]
-                    )
-                    groupeds[u].append(part)
             issue()
 
         def quantize_unit(u):
-            width = H // len(groupeds[u])
-            for i, part in enumerate(groupeds[u]):
-                cols = slice(i * width, (i + 1) * width)
-                nc.vector.quantize_mx(out=wc[u][:, cols].bitcast(FP8X4), scales=ws[u][:, cols], in_=part[:])
+            e, r = divmod(u, 4)
+            if r < 2:
+                nc.vector.quantize_mx(out=wc[u][:].bitcast(FP8X4), scales=ws[u][:], in_=groupeds[u][:])
+            elif r == 3:
+                for half in range(2):
+                    v = 4 * e + 2 + half
+                    nc.vector.quantize_mx(out=wc[v][:].bitcast(FP8X4), scales=ws[v][:], in_=pairs[e][half][:])
 
         def first_layer(e, kind):
             for s in range(2):
@@ -143,9 +153,13 @@ def tile_routed_moe_kernel(tc, xT, w1, w3, w2, gate, offs, pos1, pos2, out):
                 banks[(e, kind, s)] = acc
                 cols = slice(s * HALF, (s + 1) * HALF)
                 for t in range(4):
-                    chans = slice(t * P, (t + 1) * P)
                     for g in range(PASSES):
-                        u = 4 * e + 2 * kind + g
+                        if kind == 0:
+                            u = 4 * e + g
+                            chans = slice(t * P, (t + 1) * P)
+                        else:
+                            u = 4 * e + 2 + t // 2
+                            chans = slice((2 * g + t % 2) * P, (2 * g + t % 2 + 1) * P)
                         nc.tensor.matmul_mx(
                             out=acc[:, t, :],
                             lhsT=wc[u][:, chans].bitcast(FP8X4),

@@ -190,16 +190,17 @@ def tile_routed_moe_kernel(tc, xT, w1, w3, w2, gate, offs, pos1, pos2, out):
                 out=hc[e][:].bitcast(FP8X4), scales=hs[e][:], in_=hbs[e][:].rearrange("p n t -> p (n t)")
             )
 
-        w2c = keep.tile([P, E * N], U32, name="w2c", align_bytes=64)
-        w2s = keep.tile([P, E * N], U8, name="w2s", align_bytes=64)
+        w2c = [keep.tile([P, E * N // 2], U32, name="w2c%d" % i, align_bytes=64) for i in range(2)]
+        w2s = [keep.tile([P, E * N // 2], U8, name="w2s%d" % i, align_bytes=64) for i in range(2)]
 
         def second_weights():
-            grouped2 = stage.tile([P, PACK * E * N], BF16, name="grouped", tag="grouped", align_bytes=64)
             src2 = raws[PASSES + UNITS][:].rearrange("p e (j c i) -> p e c j i", j=PACK, i=4)
-            dst2 = grouped2[:].rearrange("p (e c i j) -> p e c j i", e=E, i=4, j=PACK)
-            nc.scalar.copy(out=dst2[:, :2], in_=src2[:, :2])
-            nc.vector.tensor_copy(out=dst2[:, 2:], in_=src2[:, 2:])
-            nc.vector.quantize_mx(out=w2c[:].bitcast(FP8X4), scales=w2s[:], in_=grouped2[:])
+            for i in (1, 0):
+                grouped2 = stage.tile([P, PACK * E * N // 2], BF16, name="grouped", tag="grouped", align_bytes=64)
+                dst2 = grouped2[:].rearrange("p (e c i j) -> p e c j i", e=E // 2, i=4, j=PACK)
+                engine_copy = (nc.scalar.copy, nc.vector.tensor_copy)[i]
+                engine_copy(out=dst2, in_=src2[:, 2 * i : 2 * i + 2])
+                nc.vector.quantize_mx(out=w2c[i][:].bitcast(FP8X4), scales=w2s[i][:], in_=grouped2[:])
 
         gather_expert(0)
 
@@ -228,11 +229,11 @@ def tile_routed_moe_kernel(tc, xT, w1, w3, w2, gate, offs, pos1, pos2, out):
 
         y_sb = keep.tile([P, E * C], F32, name="y_sb")
         for e in range(E):
-            y_ps = psum.tile([P, C], F32, name="y_ps", tag="y_ps")
+            y_ps = psum.tile([P, C], F32, name="y_ps", tag="y_ps", bufs=E)
             nc.tensor.matmul_mx(
                 out=y_ps[:],
-                lhsT=w2c[:, e * N : (e + 1) * N].bitcast(FP8X4),
-                lhsT_scale=w2s[:, e * N : (e + 1) * N],
+                lhsT=w2c[e // 2][:, (e % 2) * N : (e % 2 + 1) * N].bitcast(FP8X4),
+                lhsT_scale=w2s[e // 2][:, (e % 2) * N : (e % 2 + 1) * N],
                 rhs=hc[e][:].bitcast(FP8X4),
                 rhs_scale=hs[e][:],
                 start=True,

@@ -34,7 +34,7 @@ def tile_routed_moe_kernel(tc, xT, w1, w3, w2, gate, offs, pos1, pos2, out):
     with ExitStack() as ctx:
         lists = ctx.enter_context(tc.tile_pool(name="lists", bufs=1))
         keep = ctx.enter_context(tc.tile_pool(name="keep", bufs=1))
-        ring = ctx.enter_context(tc.tile_pool(name="ring", bufs=RAW_BUFS))
+        ring = ctx.enter_context(tc.tile_pool(name="ring", bufs=RAW_BUFS - 1))
         stage = ctx.enter_context(tc.tile_pool(name="stage", bufs=STAGE_BUFS))
         hidden = ctx.enter_context(tc.tile_pool(name="hidden", bufs=2))
         psum = ctx.enter_context(tc.psum_pool(name="psum", bufs=2))
@@ -60,7 +60,10 @@ def tile_routed_moe_kernel(tc, xT, w1, w3, w2, gate, offs, pos1, pos2, out):
 
         def issue():
             if len(raws) < len(sources):
-                raw = ring.tile([P, PACK, 512], F32, name="raw", tag="raw")
+                if len(raws) % RAW_BUFS == (PASSES + UNITS - 1) % RAW_BUFS:
+                    raw = ring.tile([P, PACK, 512], F32, name="raw_tail", tag="tail", bufs=1)
+                else:
+                    raw = ring.tile([P, PACK, 512], F32, name="raw", tag="raw")
                 nc.sync.dma_start(out=raw[:], in_=sources[len(raws)])
                 raws.append(raw)
                 if len(raws) == len(sources):
@@ -110,6 +113,7 @@ def tile_routed_moe_kernel(tc, xT, w1, w3, w2, gate, offs, pos1, pos2, out):
         hs = [keep.tile([P, C], U8, name="hs%d" % e, align_bytes=64) for e in range(E)]
         groupeds = {}
         pairs = {}
+        ga_last = []
         banks = {}
         gelus = {}
         hbs = {}
@@ -129,7 +133,7 @@ def tile_routed_moe_kernel(tc, xT, w1, w3, w2, gate, offs, pos1, pos2, out):
                         for half in range(2)
                     ]
                 for half in range(2):
-                    engine_copy = nc.vector.tensor_copy if (g == 1 or (half == 0 and V_THIRD)) else nc.scalar.copy
+                    engine_copy = nc.vector.tensor_copy if ((g == 1 and (half == 0 or u < UNITS - 1)) or (half == 0 and V_THIRD)) else nc.scalar.copy
                     engine_copy(
                         out=pairs[e][half][:, g * PACK * H // 2 : (g + 1) * PACK * H // 2].rearrange(
                             "p (t m j) -> p m j t", t=2, j=PACK
@@ -171,8 +175,13 @@ def tile_routed_moe_kernel(tc, xT, w1, w3, w2, gate, offs, pos1, pos2, out):
                         )
 
         def gelu(e, s):
-            ga = hidden.tile([P, HALF, 4], F32, name="ga", tag="ga", bufs=4)
-            nc.scalar.activation(out=ga[:], in_=banks[(e, 0, s)][:].rearrange("p t n -> p n t"), func=GELU)
+            if e < E - 1:
+                ga = hidden.tile([P, HALF, 4], F32, name="ga", tag="ga", bufs=4)[:]
+            else:
+                if s == 0:
+                    ga_last.append(ring.tile([P, 2, HALF, 4], F32, name="ga_last", tag="tail", bufs=1))
+                ga = ga_last[0][:, s]
+            nc.scalar.activation(out=ga, in_=banks[(e, 0, s)][:].rearrange("p t n -> p n t"), func=GELU)
             gelus[(e, s)] = ga
 
         def product(e, s):
@@ -181,7 +190,7 @@ def tile_routed_moe_kernel(tc, xT, w1, w3, w2, gate, offs, pos1, pos2, out):
             nc.vector.tensor_tensor(
                 out=hbs[e][:, s * HALF : (s + 1) * HALF, :],
                 in0=banks[(e, 1, s)][:].rearrange("p t n -> p n t"),
-                in1=gelus[(e, s)][:],
+                in1=gelus[(e, s)],
                 op=MULT,
             )
 

@@ -19,6 +19,8 @@ P = 128
 PACK = 4
 K_PASS = P * PACK
 PASSES = K // K_PASS
+PLANE = 4
+AHEAD = 2
 HALF = 128
 UNITS = 4 * E
 RAW_BUFS = 12
@@ -82,12 +84,11 @@ def tile_routed_moe_kernel(tc, xT, w1, w3, w2, gate, offs, pos1, pos2, out):
         nc.scalar.activation(out=warm_out[:], in_=warm_in[:], func=GELU)
 
         xw = [keep.tile([P, T], U32, name="xw%d" % g, align_bytes=64) for g in range(PASSES)]
-        xs = [keep.tile([P, T], U8, name="xs%d" % g, align_bytes=64) for g in range(PASSES)]
+        xs = keep.tile([P, T], U8, name="xs", align_bytes=64)
         chain = ctx.enter_context(tc.tile_pool(name="chain", bufs=1))
         gw = {}
         gs = {}
-        for g in range(PASSES):
-            nc.gpsimd.memset(xs[g][:], 0)
+        nc.gpsimd.memset(xs[:], 0)
 
         for g in range(PASSES):
             grouped = stage.tile([P, PACK * T], BF16, name="grouped", tag="grouped", align_bytes=64)
@@ -95,17 +96,20 @@ def tile_routed_moe_kernel(tc, xT, w1, w3, w2, gate, offs, pos1, pos2, out):
             dst = grouped[:].rearrange("p (c i j) -> p c j i", i=4, j=PACK)
             nc.scalar.copy(out=dst[:, :XS], in_=src[:, :XS])
             nc.vector.tensor_copy(out=dst[:, XS:], in_=src[:, XS:])
-            nc.vector.quantize_mx(out=xw[g][:].bitcast(FP8X4), scales=xs[g][:], in_=grouped[:])
+            nc.vector.quantize_mx(out=xw[g][:].bitcast(FP8X4), scales=xs[PLANE * g :, :], in_=grouped[:])
             issue()
 
         def gather_expert(e):
             entries = offs_t[:, e * C // 16 : (e + 1) * C // 16]
-            gw[e] = chain.tile([P, PASSES, C], U32, name="gw", tag="lo%d" % ((e + 1) % 2), align_bytes=64)
-            gs[e] = chain.tile([P, PASSES, C], U8, name="gs", tag="hi%d" % ((e + 1) % 2), align_bytes=64)
+            if e < AHEAD:
+                gw[e] = keep.tile([P, PASSES, C], U32, name="gw%d" % e, align_bytes=64)
+                gs[e] = keep.tile([P, C], U8, name="gs%d" % e, align_bytes=64)
+            else:
+                gw[e] = chain.tile([P, PASSES, C], U32, name="gw", tag="lo%d" % ((e - AHEAD) % 3), align_bytes=64)
+                gs[e] = chain.tile([P, C], U8, name="gs", tag="hi%d" % ((e - AHEAD) % 3), align_bytes=64)
             for g in range(PASSES):
                 nc.vector.tensor_copy(out=gw[e][:, g, :], in_=xw[g][:].indirect(entries))
-            for g in range(PASSES):
-                nc.vector.tensor_copy(out=gs[e][:, g, :], in_=xs[g][:].indirect(entries))
+            nc.vector.tensor_copy(out=gs[e][:], in_=xs[:].indirect(entries))
 
         wc = [keep.tile([P, H], U32, name="wc%d" % u, align_bytes=64) for u in range(UNITS)]
         ws = [keep.tile([P, H], U8, name="ws%d" % u, align_bytes=64) for u in range(UNITS)]
@@ -129,7 +133,7 @@ def tile_routed_moe_kernel(tc, xT, w1, w3, w2, gate, offs, pos1, pos2, out):
                 g = r - 2
                 if g == 0:
                     pairs[e] = [
-                        chain.tile([P, PACK * H], BF16, name="pair", tag=("lo%d", "hi%d")[half] % (e % 2), align_bytes=64)
+                        chain.tile([P, PACK * H], BF16, name="pair", tag=("lo%d", "hi%d")[half] % (e % 3), align_bytes=64)
                         for half in range(2)
                     ]
                 for half in range(2):
@@ -169,7 +173,7 @@ def tile_routed_moe_kernel(tc, xT, w1, w3, w2, gate, offs, pos1, pos2, out):
                             lhsT=wc[u][:, chans].bitcast(FP8X4),
                             lhsT_scale=ws[u][:, chans],
                             rhs=gw[e][:, g, cols].bitcast(FP8X4),
-                            rhs_scale=gs[e][:, g, cols],
+                            rhs_scale=gs[e][PLANE * g :, cols],
                             start=(g == 0),
                             stop=(g == PASSES - 1),
                         )
@@ -211,7 +215,8 @@ def tile_routed_moe_kernel(tc, xT, w1, w3, w2, gate, offs, pos1, pos2, out):
                 engine_copy(out=dst2, in_=src2[:, 2 * i : 2 * i + 2])
                 nc.vector.quantize_mx(out=w2c[i][:].bitcast(FP8X4), scales=w2s[i][:], in_=grouped2[:])
 
-        gather_expert(0)
+        for e in range(AHEAD):
+            gather_expert(e)
 
         for u in range(UNITS + MULT_LAG):
             if u < UNITS:
@@ -222,8 +227,8 @@ def tile_routed_moe_kernel(tc, xT, w1, w3, w2, gate, offs, pos1, pos2, out):
                     first_layer((u - 1) // 4, 0)
                 if (u - 1) % 4 == 3:
                     first_layer((u - 1) // 4, 1)
-                    if (u - 1) // 4 + 1 < E:
-                        gather_expert((u - 1) // 4 + 1)
+                    if (u - 1) // 4 + AHEAD < E:
+                        gather_expert((u - 1) // 4 + AHEAD)
             if u == UNITS:
                 second_weights()
             if u >= GELU_LAG and (u - GELU_LAG) % 4 == 0 and (u - GELU_LAG) // 4 < E:

from contextlib import ExitStack

import concourse.mybir as mybir

K, T, E, C, H, N = 1024, 512, 4, 256, 512, 128
FLOPS = 2 * E * C * (2 * K * H + H * N)

F32 = mybir.dt.float32
BF16 = mybir.dt.bfloat16
U32 = mybir.dt.uint32
U16 = mybir.dt.uint16
U8 = mybir.dt.uint8
FP8X4 = mybir.dt.float8_e4m3fn_x4
GELU = mybir.ActivationFunctionType.Gelu_apprx_tanh
MULT = mybir.AluOpType.mult
ADD = mybir.AluOpType.add

P = 128
PACK = 4
K_PASS = P * PACK
PASSES = K // K_PASS
PLANE = 4
AHEAD = 2
HALF = 128
UNITS = 4 * E
RAW_BUFS = 12
STAGE_BUFS = 8
XS = 44
GELU_LAG = 3
MULT_LAG = 5
V_THIRD = True


def tile_routed_moe_kernel(tc, xT, w1, w3, w2, gate, offs, pos1, pos2, out):
    nc = tc.nc
    with ExitStack() as ctx:
        lists = ctx.enter_context(tc.tile_pool(name="lists", bufs=1))
        keep = ctx.enter_context(tc.tile_pool(name="keep", bufs=1))
        ring = ctx.enter_context(tc.tile_pool(name="ring", bufs=RAW_BUFS - 1))
        stage = ctx.enter_context(tc.tile_pool(name="stage", bufs=STAGE_BUFS))
        hidden = ctx.enter_context(tc.tile_pool(name="hidden", bufs=2))
        psum = ctx.enter_context(tc.psum_pool(name="psum", bufs=2))

        offs_t = lists.tile([P, E * C // 16], U16, name="offs_t")
        nc.sync.dma_start(offs_t[:], offs)
        pos1_t = lists.tile([P, T // 16], U16, name="pos1_t")
        pos2_t = lists.tile([P, T // 16], U16, name="pos2_t")

        x_view = xT.rearrange("(g p j) n -> g p j n", p=P, j=PACK)
        w_views = (
            w1.rearrange("e (g p j) c -> e g p j c", p=P, j=PACK),
            w3.rearrange("e (g p j) c -> e g p j c", p=P, j=PACK),
        )
        sources = [x_view[g] for g in range(PASSES)]
        for e in range(E):
            for kind in range(2):
                for g in range(PASSES):
                    sources.append(w_views[kind][e, g])
        sources.append(w2.rearrange("e (p j) n -> p e (j n)", j=PACK))
        raws = []
        gates = []

        def issue():
            if len(raws) < len(sources):
                if len(raws) % RAW_BUFS == (PASSES + UNITS - 1) % RAW_BUFS:
                    raw = ring.tile([P, PACK, 512], F32, name="raw_tail", tag="tail", bufs=1)
                else:
                    raw = ring.tile([P, PACK, 512], F32, name="raw", tag="raw")
                nc.sync.dma_start(out=raw[:], in_=sources[len(raws)])
                raws.append(raw)
                if len(raws) == len(sources):
                    nc.sync.dma_start(pos1_t[:], pos1)
                    nc.sync.dma_start(pos2_t[:], pos2)
                    gate_t = ring.tile([P, 2, T], F32, name="raw", tag="raw")
                    nc.sync.dma_start(out=gate_t[:], in_=gate.rearrange("r n t -> n r t"))
                    gates.append(gate_t)

        for i in range(RAW_BUFS):
            issue()

        warm_in = keep.tile([P, 1], F32, name="warm_in")
        warm_out = keep.tile([P, 1], F32, name="warm_out")
        nc.vector.memset(warm_in[:], 0.0)
        nc.scalar.activation(out=warm_out[:], in_=warm_in[:], func=GELU)

        xw = [keep.tile([P, T], U32, name="xw%d" % g, align_bytes=64) for g in range(PASSES)]
        xs = keep.tile([P, T], U8, name="xs", align_bytes=64)
        chain = ctx.enter_context(tc.tile_pool(name="chain", bufs=1))
        gw = {}
        gs = {}
        nc.gpsimd.memset(xs[:], 0)

        for g in range(PASSES):
            grouped = stage.tile([P, PACK * T], BF16, name="grouped", tag="grouped", align_bytes=64)
            src = raws[g][:].rearrange("p j (c i) -> p c j i", i=4)
            dst = grouped[:].rearrange("p (c i j) -> p c j i", i=4, j=PACK)
            nc.scalar.copy(out=dst[:, :XS], in_=src[:, :XS])
            nc.vector.tensor_copy(out=dst[:, XS:], in_=src[:, XS:])
            nc.vector.quantize_mx(out=xw[g][:].bitcast(FP8X4), scales=xs[PLANE * g :, :], in_=grouped[:])
            issue()

        def gather_expert(e):
            entries = offs_t[:, e * C // 16 : (e + 1) * C // 16]
            if e < AHEAD:
                gw[e] = keep.tile([P, PASSES, C], U32, name="gw%d" % e, align_bytes=64)
                gs[e] = keep.tile([P, C], U8, name="gs%d" % e, align_bytes=64)
            else:
                gw[e] = chain.tile([P, PASSES, C], U32, name="gw", tag="lo%d" % ((e - AHEAD) % 3), align_bytes=64)
                gs[e] = chain.tile([P, C], U8, name="gs", tag="hi%d" % ((e - AHEAD) % 3), align_bytes=64)
            for g in range(PASSES):
                nc.vector.tensor_copy(out=gw[e][:, g, :], in_=xw[g][:].indirect(entries))
            nc.vector.tensor_copy(out=gs[e][:], in_=xs[:].indirect(entries))

        wc = [keep.tile([P, H], U32, name="wc%d" % u, align_bytes=64) for u in range(UNITS)]
        ws = [keep.tile([P, H], U8, name="ws%d" % u, align_bytes=64) for u in range(UNITS)]
        hc = [keep.tile([P, C], U32, name="hc%d" % e, align_bytes=64) for e in range(E)]
        hs = [keep.tile([P, C], U8, name="hs%d" % e, align_bytes=64) for e in range(E)]
        groupeds = {}
        pairs = {}
        ga_last = []
        banks = {}
        gelus = {}
        hbs = {}

        def copy_unit(u):
            src = raws[PASSES + u][:].rearrange("p j (m t) -> p m j t", t=4)
            e, r = divmod(u, 4)
            if r < 2:
                grouped = stage.tile([P, PACK * H], BF16, name="grouped", tag="grouped", align_bytes=64)
                nc.scalar.copy(out=grouped[:].rearrange("p (t m j) -> p m j t", t=4, j=PACK), in_=src)
                groupeds[u] = grouped
            else:
                g = r - 2
                if g == 0:
                    pairs[e] = [
                        chain.tile([P, PACK * H], BF16, name="pair", tag=("lo%d", "hi%d")[half] % (e % 3), align_bytes=64)
                        for half in range(2)
                    ]
                for half in range(2):
                    engine_copy = nc.vector.tensor_copy if ((g == 1 and (half == 0 or u < UNITS - 1)) or (half == 0 and V_THIRD)) else nc.scalar.copy
                    engine_copy(
                        out=pairs[e][half][:, g * PACK * H // 2 : (g + 1) * PACK * H // 2].rearrange(
                            "p (t m j) -> p m j t", t=2, j=PACK
                        ),
                        in_=src[:, :, :, 2 * half : 2 * half + 2],
                    )
            issue()

        def quantize_unit(u):
            e, r = divmod(u, 4)
            if r < 2:
                nc.vector.quantize_mx(out=wc[u][:].bitcast(FP8X4), scales=ws[u][:], in_=groupeds[u][:])
            elif r == 3:
                for half in range(2):
                    v = 4 * e + 2 + half
                    nc.vector.quantize_mx(out=wc[v][:].bitcast(FP8X4), scales=ws[v][:], in_=pairs[e][half][:])

        def first_layer(e, kind):
            for s in range(2):
                acc = psum.tile([P, 4, HALF], F32, name="acc%d" % kind, tag="acc%d" % kind)
                banks[(e, kind, s)] = acc
                cols = slice(s * HALF, (s + 1) * HALF)
                for t in range(4):
                    for g in range(PASSES):
                        if kind == 0:
                            u = 4 * e + g
                            chans = slice(t * P, (t + 1) * P)
                        else:
                            u = 4 * e + 2 + t // 2
                            chans = slice((2 * g + t % 2) * P, (2 * g + t % 2 + 1) * P)
                        nc.tensor.matmul_mx(
                            out=acc[:, t, :],
                            lhsT=wc[u][:, chans].bitcast(FP8X4),
                            lhsT_scale=ws[u][:, chans],
                            rhs=gw[e][:, g, cols].bitcast(FP8X4),
                            rhs_scale=gs[e][PLANE * g :, cols],
                            start=(g == 0),
                            stop=(g == PASSES - 1),
                        )

        def gelu(e, s):
            if e < E - 1:
                ga = hidden.tile([P, HALF, 4], F32, name="ga", tag="ga", bufs=4)[:]
            else:
                if s == 0:
                    ga_last.append(ring.tile([P, 2, HALF, 4], F32, name="ga_last", tag="tail", bufs=1))
                ga = ga_last[0][:, s]
            nc.scalar.activation(out=ga, in_=banks[(e, 0, s)][:].rearrange("p t n -> p n t"), func=GELU)
            gelus[(e, s)] = ga

        def product(e, s):
            if s == 0:
                hbs[e] = hidden.tile([P, C, 4], BF16, name="hb", tag="hb", align_bytes=64)
            nc.vector.tensor_tensor(
                out=hbs[e][:, s * HALF : (s + 1) * HALF, :],
                in0=banks[(e, 1, s)][:].rearrange("p t n -> p n t"),
                in1=gelus[(e, s)],
                op=MULT,
            )

        def quantize_hidden(e):
            nc.vector.quantize_mx(
                out=hc[e][:].bitcast(FP8X4), scales=hs[e][:], in_=hbs[e][:].rearrange("p n t -> p (n t)")
            )

        w2c = [keep.tile([P, E * N // 2], U32, name="w2c%d" % i, align_bytes=64) for i in range(2)]
        w2s = [keep.tile([P, E * N // 2], U8, name="w2s%d" % i, align_bytes=64) for i in range(2)]

        def second_weights():
            src2 = raws[PASSES + UNITS][:].rearrange("p e (j c i) -> p e c j i", j=PACK, i=4)
            for i in (1, 0):
                grouped2 = stage.tile([P, PACK * E * N // 2], BF16, name="grouped", tag="grouped", align_bytes=64)
                dst2 = grouped2[:].rearrange("p (e c i j) -> p e c j i", e=E // 2, i=4, j=PACK)
                engine_copy = (nc.scalar.copy, nc.vector.tensor_copy)[i]
                engine_copy(out=dst2, in_=src2[:, 2 * i : 2 * i + 2])
                nc.vector.quantize_mx(out=w2c[i][:].bitcast(FP8X4), scales=w2s[i][:], in_=grouped2[:])

        for e in range(AHEAD):
            gather_expert(e)

        for u in range(UNITS + MULT_LAG):
            if u < UNITS:
                copy_unit(u)
            if 1 <= u <= UNITS:
                quantize_unit(u - 1)
                if (u - 1) % 4 == 1:
                    first_layer((u - 1) // 4, 0)
                if (u - 1) % 4 == 3:
                    first_layer((u - 1) // 4, 1)
                    if (u - 1) // 4 + AHEAD < E:
                        gather_expert((u - 1) // 4 + AHEAD)
            if u == UNITS:
                second_weights()
            if u >= GELU_LAG and (u - GELU_LAG) % 4 == 0 and (u - GELU_LAG) // 4 < E:
                gelu((u - GELU_LAG) // 4, 0)
                gelu((u - GELU_LAG) // 4, 1)
            if u >= MULT_LAG and (u - MULT_LAG) % 4 == 0:
                product((u - MULT_LAG) // 4, 0)
            if u >= MULT_LAG + 1 and (u - MULT_LAG - 1) % 4 == 0:
                product((u - MULT_LAG - 1) // 4, 1)
            if u >= MULT_LAG + 2 and (u - MULT_LAG - 2) % 4 == 0:
                quantize_hidden((u - MULT_LAG - 2) // 4)

        y_sb = keep.tile([P, E * C], F32, name="y_sb")
        for e in range(E):
            y_ps = psum.tile([P, C], F32, name="y_ps", tag="y_ps", bufs=E)
            nc.tensor.matmul_mx(
                out=y_ps[:],
                lhsT=w2c[e // 2][:, (e % 2) * N : (e % 2 + 1) * N].bitcast(FP8X4),
                lhsT_scale=w2s[e // 2][:, (e % 2) * N : (e % 2 + 1) * N],
                rhs=hc[e][:].bitcast(FP8X4),
                rhs_scale=hs[e][:],
                start=True,
                stop=True,
            )
            nc.scalar.copy(out=y_sb[:, e * C : (e + 1) * C], in_=y_ps[:])

        first = keep.tile([P, T], F32, name="first")
        second = keep.tile([P, T], F32, name="second")
        total = keep.tile([P, T], F32, name="total")
        nc.vector.tensor_tensor(out=first[:], in0=y_sb[:].indirect(pos1_t[:]), in1=gates[0][:, 0, :], op=MULT)
        nc.vector.tensor_tensor(out=second[:], in0=y_sb[:].indirect(pos2_t[:]), in1=gates[0][:, 1, :], op=MULT)
        nc.vector.tensor_tensor(out=total[:], in0=first[:], in1=second[:], op=ADD)
        nc.sync.dma_start(out=out, in_=total[:])
